import numpy as np
import ml_dtypes

BF16 = ml_dtypes.bfloat16


def bf(x):
    return np.asarray(x, np.float32).astype(BF16)


def f32(x):
    return np.asarray(x, np.float32)


def f64(x):
    return np.asarray(x).astype(np.float64)


def striped(idx):
    return np.concatenate([l.reshape(-1, 16).T for l in idx])


def rows(idx, k):
    return np.tile(np.repeat(idx, 16, axis=0), (k // (16 * 8), 1))


def look(tab, idx):
    return np.take_along_axis(f64(tab), rows(idx, len(tab)), axis=1)


K, S, V, N = 256, 2048, 512, 512


def setup_inputs():
    return {"tab": f32(np.random.standard_normal((K, S))), "pos": f32(np.random.standard_normal((K, V))), "offs": striped(np.stack([np.random.permutation(S)[:N] for _ in range(8)]))}


def reference(tab, pos, offs):
    idx = np.stack([g.T.reshape(-1) for g in np.split(offs, 8)])
    x = np.maximum(look(tab, idx) - f64(pos) + 0.5, 0.0)
    return x

import concourse.mybir as mybir

F32 = mybir.dt.float32
U16 = mybir.dt.uint16
ALU = mybir.AluOpType

P = 128
MARGIN = 0.5


def tile_lookup_hinge_sub_out_kernel(tc, tab, pos, offs, out):
    nc = tc.nc
    rows, window_columns = tab.shape
    n = pos.shape[1]
    with tc.tile_pool(name="held", bufs=1) as held:
        lists = held.tile([P, n // 16], U16, name="lists")
        nc.sync.dma_start(lists[:], offs)

        for b in range(rows // P):
            block = slice(b * P, (b + 1) * P)
            window = held.tile([P, window_columns], F32, name=f"window{b}")
            positives = held.tile([P, n], F32, name=f"positives{b}")
            difference = held.tile([P, n], F32, name=f"difference{b}")
            hinge = held.tile([P, n], F32, name=f"hinge{b}")

            nc.sync.dma_start(window[:], tab[block, :])
            nc.scalar.dma_start(positives[:], pos[block, :])
            nc.vector.tensor_tensor(difference[:], window[:].indirect(lists[:]), positives[:], ALU.subtract)
            nc.vector.tensor_scalar(hinge[:], difference[:], MARGIN, 0.0, ALU.add, ALU.max)
            nc.scalar.dma_start(out[block, :], hinge[:])
